import numpy as np
import ml_dtypes


def mxq(x, axis, fmt="e4m3"):
    dtype, down = {"e4m3": (ml_dtypes.float8_e4m3fn, 7), "e5m2": (ml_dtypes.float8_e5m2, 14)}[fmt]
    v = np.moveaxis(np.asarray(x, np.float32).astype(ml_dtypes.bfloat16).astype(np.float64), axis, -1)
    blocks = v.reshape(v.shape[:-1] + (-1, 32))
    amax = np.abs(blocks).max(-1, keepdims=True)
    byte = np.maximum(np.where(amax > 0, np.frexp(amax)[1] - 1 + 127, 0) - down, 1)
    scale = np.exp2(byte - 127.0)
    codes = (blocks / scale).astype(np.float32).astype(dtype).astype(np.float64)
    return np.moveaxis((codes * scale).reshape(v.shape), -1, axis)


WIDE = False


def mx_kscale(k):
    if not WIDE:
        return np.ones(k)
    levels = np.array([10, -10, 5, -5, 0])
    if k % 512:
        return np.exp2(np.random.permutation(np.resize(levels, k // 32))).repeat(32)
    a = np.empty((k // 512, 16))
    for p in range(k // 512):
        a[p, :8] = np.random.permutation(np.resize(levels, 8))
        for g in range(8):
            far = levels[np.abs(levels - a[p, g]) >= 10]
            a[p, g + 8] = far[np.random.randint(len(far))]
    return np.exp2(a.ravel()).repeat(32)


def f64(x):
    return np.asarray(x).astype(np.float64)


def striped(idx):
    return np.tile(idx.reshape(-1, 16).T, (8, 1)).astype(np.uint16)


def unstriped(offs):
    return offs[:16].T.reshape(-1).astype(np.int64)


def striped8(idx):
    return np.concatenate([x.reshape(-1, 16).T for x in idx]).astype(np.uint16)


def runs(offs, k):
    lists = np.stack([offs[16 * r : 16 * r + 16].T.reshape(-1) for r in range(8)]).astype(np.int64)
    return lists[np.arange(k) % 512 // 64]


def pack_weight(w):
    k, n = w.shape
    w = f64(np.asarray(w, np.float32).astype(ml_dtypes.bfloat16)).reshape(k // 32, 32, n)
    amax = np.abs(w).max(1)
    byte = np.clip(np.where(amax > 0, np.frexp(amax)[1] - 1 + 127 - 7, 1), 1, 254)
    scaled = (w * np.exp2(127.0 - byte)[:, None, :]).reshape(k, n).astype(np.float32)
    words = np.ascontiguousarray(scaled.reshape(k // 512, 128, 4, n).transpose(0, 1, 3, 2)).astype(ml_dtypes.float8_e4m3fn).view(np.uint8)
    return words, np.ascontiguousarray(byte.astype(np.uint8).reshape(k // 512, 16, n))


def unpack_weight(words, scales):
    g, p, n, _ = words.shape
    vals = np.ascontiguousarray(words).view(ml_dtypes.float8_e4m3fn).astype(np.float64) * np.repeat(np.exp2(scales.astype(np.float64) - 127.0), 8, axis=1)[..., None]
    return vals.transpose(0, 1, 3, 2).reshape(g * 512, n)


K, T, S, N, H = 512, 2048, 512, 512, 512


def setup_inputs():
    n = np.random.standard_normal
    s = mx_kscale(K)[:, None]
    u = mx_kscale(H)
    packed_xT = pack_weight(n((K, T)) * s)
    return {
        "x_words": packed_xT[0],
        "x_scales": packed_xT[1],
        "w1": (n((K, H)) / np.sqrt(K) / s).astype(np.float32),
        "gn": (np.random.uniform(0.5, 1.5, (H, 1)) * u[:, None]).astype(np.float32),
        "w2": (n((H, N)) / np.sqrt(H) / u[:, None]).astype(np.float32),
        "w3": (n((K, N)) / np.sqrt(K) / s).astype(np.float32),
        "offs": striped(np.random.permutation(T)[:S]),
        "n1": striped8(np.stack([np.random.permutation(S) for _ in range(8)])),
        "n2": striped8(np.stack([np.random.permutation(S) for _ in range(8)])),
        "two": striped(np.random.permutation(T)[:S]),
        "n3": striped8(np.stack([np.random.permutation(S) for _ in range(8)])),
        "n4": striped8(np.stack([np.random.permutation(S) for _ in range(8)])),
    }


def reference(x_words, x_scales, w1, gn, w2, w3, offs, n1, n2, two, n3, n4):
    xq = unpack_weight(x_words, x_scales)[:, unstriped(offs)]
    y = mxq(f64(w1), 0, "e4m3").T @ xq
    ex = np.exp(y)
    z = f64(gn) * (np.log(ex + ex[np.arange(H)[:, None], runs(n1, H)]) - (y[np.arange(H)[:, None], runs(n2, H)]))
    h = mxq(f64(w2), 0, "e4m3").T @ mxq(z, 0, "e4m3")
    x_two = unpack_weight(x_words, x_scales)[:, unstriped(two)]
    d = mxq(f64(w3), 0, "e4m3").T @ x_two
    return 0.75 * (h * (d[np.arange(N)[:, None], runs(n4, N)]) - ((h[np.arange(N)[:, None], runs(n3, N)]) * d))

@@ -1,0 +1,291 @@
+from contextlib import ExitStack
+
+import concourse.mybir as mybir
+from concourse.masks import make_identity
+
+K, T, S, H, N = 512, 2048, 512, 512, 512
+FLOPS = 2 * S * (K * H + H * N + K * N)
+
+F32 = mybir.dt.float32
+BF16 = mybir.dt.bfloat16
+I32 = mybir.dt.int32
+U32 = mybir.dt.uint32
+U16 = mybir.dt.uint16
+U8 = mybir.dt.uint8
+FP8X4 = mybir.dt.float8_e4m3fn_x4
+ACT = mybir.ActivationFunctionType
+ALU = mybir.AluOpType
+
+P = 128
+PACK = 4
+HALF = S // 2
+WINDOW = 2 * S
+
+
+def tile_picked_latecrossblse_none_p_kernel(tc, x_words, x_scales, w1, gn, w2, w3, offs, n1, n2, two, n3, n4, out):
+    nc = tc.nc
+    with ExitStack() as ctx:
+        sb = ctx.enter_context(tc.tile_pool(name="sb", bufs=1))
+        psum = ctx.enter_context(tc.psum_pool(name="psum", bufs=1))
+
+        def load_list(src, name):
+            tile = sb.tile([P, S // 16], U16, name=name)
+            nc.sync.dma_start(tile[:], src)
+            return tile
+
+        def load_weight(w, name):
+            raw = sb.tile([P, PACK, S], F32, name=name)
+            nc.sync.dma_start(raw[:], w.rearrange("(p j) c -> p j c", j=PACK))
+            return raw
+
+        scale_table = sb.tile([P, T], U8, name="scale_table")
+        nc.gpsimd.memset(scale_table[:].bitcast(I32), 0)
+        offs_t = load_list(offs, "offs_t")
+        two_t = load_list(two, "two_t")
+        for q in range(4):
+            nc.sync.dma_start(scale_table[32 * q : 32 * q + 4, :].bitcast(I32), x_scales[0, 4 * q : 4 * q + 4, :].bitcast(I32))
+        w1_raw = load_weight(w1, "w1_raw")
+        word_table = sb.tile([P, T], I32, name="word_table")
+        nc.sync.dma_start(word_table[:], x_words[0].rearrange("p n t -> p (n t)").bitcast(I32))
+        n1_t = load_list(n1, "n1_t")
+        gain = sb.tile([P, PACK], F32, name="gain")
+        nc.sync.dma_start(gain[:], gn.rearrange("(p t) o -> p (t o)", t=PACK))
+        w3_raw = load_weight(w3, "w3_raw")
+        n2_t = load_list(n2, "n2_t")
+        w2_raw = load_weight(w2, "w2_raw")
+        n4_t = load_list(n4, "n4_t")
+        n3_t = load_list(n3, "n3_t")
+        identity = sb.tile([P, P], F32, name="identity")
+        make_identity(nc, identity[:])
+
+        def pick_scales(lst, name):
+            picked = sb.tile([P, S], U8, name=name, align_bytes=64)
+            nc.vector.tensor_copy(picked[:], scale_table[:].indirect(lst[:]))
+            return picked
+
+        def pick_words(lst, name, pieces):
+            picked = sb.tile([P, S], U32, name=name, align_bytes=64)
+            for cols in pieces:
+                nc.vector.tensor_copy(picked[:, cols], word_table[:].bitcast(U32).indirect(lst[:, cols.start // 16 : cols.stop // 16]))
+            return picked
+
+        def deal(raw, u, on_scalar, tag):
+            grouped = sb.tile([P, 2, P, PACK], BF16, name="grouped", tag=tag, align_bytes=64)
+            dst = grouped[:].rearrange("p t m j -> p m j t")
+            src = raw[:].rearrange("p j (m t) -> p m j t", t=PACK)[:, :, :, 2 * u : 2 * u + 2]
+            if on_scalar:
+                nc.scalar.activation(dst, src, ACT.Copy)
+            else:
+                nc.vector.tensor_copy(dst, src)
+            return grouped
+
+        def mx_tiles(name):
+            codes = sb.tile([P, S], U32, name=name + "_codes", align_bytes=64)
+            scales = sb.tile([P, S], U8, name=name + "_scales", align_bytes=64)
+            return codes, scales
+
+        def quantize(operand, cols, values):
+            nc.vector.quantize_mx(out=operand[0][:, cols].bitcast(FP8X4), scales=operand[1][:, cols], in_=values)
+
+        def product(acc, weights, t, moving, cols):
+            rows = slice(t * P, (t + 1) * P)
+            nc.tensor.matmul_mx(
+                out=acc[:, cols],
+                lhsT=weights[0][:, rows].bitcast(FP8X4), lhsT_scale=weights[1][:, rows],
+                rhs=moving[0][:, cols].bitcast(FP8X4), rhs_scale=moving[1][:, cols],
+                start=True, stop=True,
+            )
+
+        def turn(bank, span, *terms):
+            for first_col in range(span.start, span.stop, P):
+                cols = slice(first_col, first_col + P)
+                for k, term in enumerate(terms):
+                    nc.tensor.matmul(bank[:, cols], term[:, cols], identity[:], start=k == 0, stop=k == len(terms) - 1, is_transpose=True)
+
+        def bank_a(t):
+            return psum.tile([P, S], F32, name="bank_a%d" % t)
+
+        def bank_b(t):
+            return psum.tile([P, S], F32, name="bank_b%d" % t)
+
+        every = slice(0, S)
+        halves = [slice(0, HALF), slice(HALF, S)]
+
+        x1_scales = pick_scales(offs_t, "x1_scales")
+        x2_scales = pick_scales(two_t, "x2_scales")
+        w1_g = [deal(w1_raw, 0, False, "w1_a"), deal(w1_raw, 1, True, "w1_b")]
+        w1_q = mx_tiles("w1")
+        for u in range(2):
+            quantize(w1_q, halves[u], w1_g[u][:].rearrange("p t m j -> p (t m j)"))
+        x1 = (pick_words(offs_t, "x1_words", halves), x1_scales)
+        x2 = (pick_words(two_t, "x2_words", [every]), x2_scales)
+        y_ps = [bank_a(t) for t in range(PACK)]
+        ex_win, sum_ps = [], []
+        left, right = halves
+        for t in range(2):
+            product(y_ps[t], w1_q, t, x1, left)
+        for t in range(PACK):
+            product(y_ps[t], w1_q, t, x1, right if t < 2 else every)
+            ex_win.append(sb.tile([P, WINDOW], F32, name="ex_win%d" % t))
+            nc.scalar.activation(ex_win[t][:, :S], y_ps[t][:], ACT.Exp)
+
+        for t in range(PACK):
+            ex_far = sb.tile([P, S], F32, name="ex_far%d" % t, align_bytes=64)
+            nc.vector.tensor_copy(ex_far[:], ex_win[t][:].indirect(n1_t[:]))
+            sum_ps.append(bank_b(t))
+            turn(sum_ps[t], every, ex_win[t], ex_far)
+
+        w3_g = [deal(w3_raw, 0, False, "ex_far1"), deal(w3_raw, 1, False, "ex_far2")]
+        w3_q = mx_tiles("w3")
+        for u in range(2):
+            quantize(w3_q, halves[u], w3_g[u][:].rearrange("p t m j -> p (t m j)"))
+
+        w2_q = mx_tiles("w2")
+        w2_left = deal(w2_raw, 0, False, "ex_far3")
+        quantize(w2_q, left, w2_left[:].rearrange("p t m j -> p (t m j)"))
+
+        last = PACK - 1
+        neg_z = sb.tile([P, PACK, S], F32, name="neg_z")
+        d_ps, gy_win, glse = [], [], []
+
+        def subtract_far(t, cols):
+            lc = slice(cols.start // 16, cols.stop // 16)
+            nc.vector.tensor_tensor(neg_z[:, t, cols], gy_win[t][:].indirect(n2_t[:, lc]), glse[t][:, cols], ALU.subtract)
+
+        lse_ps = []
+
+        def logarithm(t):
+            lse_turned = sb.tile([P, S], F32, name="lse_turned%d" % t, align_bytes=64)
+            nc.scalar.activation(lse_turned[:], sum_ps[t][:], ACT.Ln)
+            lse_ps.append(bank_b(t))
+            turn(lse_ps[t], every, lse_turned)
+
+        logarithm(0)
+        for t in range(PACK):
+            gy_win.append(sb.tile([P, WINDOW], F32, name="gy_win%d" % t))
+            nc.scalar.activation(gy_win[t][:, :S], y_ps[t][:], ACT.Copy, scale=gain[:, t : t + 1])
+            if t != last:
+                logarithm(t + 1)
+            glse.append(sb.tile([P, S], F32, name="glse%d" % t))
+            nc.scalar.activation(glse[t][:], lse_ps[t][:], ACT.Copy, scale=gain[:, t : t + 1])
+            if t != last:
+                subtract_far(t, every)
+        for t in range(PACK):
+            d_ps.append(bank_a(t))
+            product(d_ps[t], w3_q, t, x2, every)
+        w2_right = deal(w2_raw, 1, True, "lse_turned3")
+
+        d_win = [sb.tile([P, WINDOW], F32, name="d_win%d" % t) for t in range(PACK)]
+        h_win = [sb.tile([P, WINDOW], F32, name="h_win%d" % t) for t in range(PACK)]
+
+        def d_out(t, negated):
+            if negated:
+                nc.scalar.activation(d_win[t][:, S:], d_ps[t][:], ACT.Copy, scale=0.75)
+            else:
+                nc.scalar.activation(d_win[t][:, :S], d_ps[t][:], ACT.Copy, scale=-0.75)
+
+        z_q = mx_tiles("z")
+
+        def weave(cols):
+            woven = sb.tile([P, HALF, PACK], BF16, name="woven", align_bytes=64)
+            nc.vector.tensor_copy(
+                woven[:].rearrange("p (c i) t -> p c t i", i=4),
+                neg_z[:, :, cols].rearrange("p t (c i) -> p c t i", i=4),
+            )
+            return woven[:].rearrange("p c t -> p (c t)")
+
+        h_ps = {}
+
+        def h_out(t, cols):
+            if t not in h_ps:
+                h_ps.setdefault(t, bank_b(t))
+            product(h_ps[t], w2_q, t, z_q, cols)
+            nc.scalar.activation(h_win[t][:, cols], h_ps[t][:, cols], ACT.Copy)
+
+        d_out(0, False)
+        d_out(0, True)
+        d_out(1, False)
+        subtract_far(last, left)
+        z_left = weave(left)
+        subtract_far(last, right)
+        quantize(z_q, left, z_left)
+        h_out(0, left)
+        h_out(1, left)
+        z_right = weave(right)
+        quantize(w2_q, right, w2_right[:].rearrange("p t m j -> p (t m j)"))
+        quantize(z_q, right, z_right)
+        h_out(0, right)
+        h_out(1, right)
+        d_out(1, True)
+
+        out_rows = out.rearrange("(p t) n -> t p n", t=PACK)
+        first = [sb.tile([P, S], F32, name="first%d" % t) for t in range(PACK)]
+        second = [sb.tile([P, S], F32, name="second%d" % t) for t in range(PACK)]
+        res = [sb.tile([P, S], F32, name="res%d" % t) for t in range(PACK)]
+
+        def first_term(t, cols):
+            lc = slice(cols.start // 16, cols.stop // 16)
+            nc.vector.tensor_tensor(first[t][:, cols], d_win[t][:].indirect(n4_t[:, lc]), h_win[t][:, cols], ALU.mult)
+
+        def second_term(t, cols):
+            lc = slice(cols.start // 16, cols.stop // 16)
+            shift = 0 if t == last else S
+            nc.vector.tensor_tensor(second[t][:, cols], h_win[t][:].indirect(n3_t[:, lc]), d_win[t][:, shift + cols.start : shift + cols.stop], ALU.mult)
+
+        turned = [sb.tile([P, S], F32, name="turned%d" % t) for t in range(last)]
+        turned_ps, res_ps = {}, {}
+
+        def add_terms(t, cols):
+            if t not in turned_ps:
+                turned_ps.setdefault(t, bank_a(t))
+            turn(turned_ps[t], cols, first[t], second[t])
+
+        def sum_out(t, cols):
+            nc.scalar.activation(turned[t][:, cols], turned_ps[t][:, cols], ACT.Copy)
+
+        def turn_back(t, cols):
+            if t not in res_ps:
+                res_ps.setdefault(t, bank_b(t))
+            turn(res_ps[t], cols, turned[t])
+
+        def store(t, cols):
+            nc.scalar.activation(res[t][:, cols], res_ps[t][:, cols], ACT.Copy)
+            nc.scalar.dma_start(out_rows[t][:, cols], res[t][:, cols])
+
+        d_out(2, False)
+        d_out(2, True)
+        h_out(2, every)
+        d_out(3, False)
+        h_out(3, every)
+        first_term(0, left)
+        first_term(1, left)
+        first_term(0, right)
+        second_term(0, every)
+        first_term(1, right)
+        second_term(1, every)
+        for cols in halves:
+            first_term(2, cols)
+            second_term(2, cols)
+        first_term(3, every)
+        for cols in halves:
+            second_term(3, cols)
+        for cols in halves:
+            nc.vector.tensor_tensor(res[3][:, cols], first[3][:, cols], second[3][:, cols], ALU.subtract)
+        add_terms(0, every)
+        sum_out(0, every)
+        add_terms(1, every)
+        turn_back(0, every)
+        sum_out(1, every)
+        store(0, every)
+        add_terms(2, left)
+        turn_back(1, every)
+        sum_out(2, left)
+        store(1, every)
+        add_terms(2, right)
+        turn_back(2, left)
+        sum_out(2, right)
+        store(2, left)
+        turn_back(2, right)
+        store(2, right)
+        for cols in halves:
+            nc.sync.dma_start(out_rows[3][:, cols], res[3][:, cols])

@@ -126,31 +126,8 @@ def tile_picked_latecrossblse_none_p_kernel(tc, x_words, x_scales, w1, gn, w2, w
             product(y_ps[t], w1_q, t, x1, left)
         for t in range(PACK):
             product(y_ps[t], w1_q, t, x1, right if t < 2 else every)
-            ex_win.append(sb.tile([P, WINDOW], F32, name="ex_win%d" % t))
+            ex_win.append(sb.tile([P, WINDOW], F32, name="ex_win%d" % t, align_bytes=64))
             nc.scalar.activation(ex_win[t][:, :S], y_ps[t][:], ACT.Exp)
-
-        for t in range(PACK):
-            ex_far = sb.tile([P, S], F32, name="ex_far%d" % t, align_bytes=64)
-            nc.vector.tensor_copy(ex_far[:], ex_win[t][:].indirect(n1_t[:]))
-            sum_ps.append(bank_b(t))
-            turn(sum_ps[t], every, ex_win[t], ex_far)
-
-        w3_g = [deal(w3_raw, 0, False, "ex_far1"), deal(w3_raw, 1, False, "ex_far2")]
-        w3_q = mx_tiles("w3")
-        for u in range(2):
-            quantize(w3_q, halves[u], w3_g[u][:].rearrange("p t m j -> p (t m j)"))
-
-        w2_q = mx_tiles("w2")
-        w2_left = deal(w2_raw, 0, False, "ex_far3")
-        quantize(w2_q, left, w2_left[:].rearrange("p t m j -> p (t m j)"))
-
-        last = PACK - 1
-        neg_z = sb.tile([P, PACK, S], F32, name="neg_z")
-        d_ps, gy_win, glse = [], [], []
-
-        def subtract_far(t, cols):
-            lc = slice(cols.start // 16, cols.stop // 16)
-            nc.vector.tensor_tensor(neg_z[:, t, cols], gy_win[t][:].indirect(n2_t[:, lc]), glse[t][:, cols], ALU.subtract)
 
         lse_ps = []
 
@@ -160,9 +137,35 @@ def tile_picked_latecrossblse_none_p_kernel(tc, x_words, x_scales, w1, gn, w2, w
             lse_ps.append(bank_b(t))
             turn(lse_ps[t], every, lse_turned)
 
-        logarithm(0)
         for t in range(PACK):
-            gy_win.append(sb.tile([P, WINDOW], F32, name="gy_win%d" % t))
+            ex_far = sb.tile([P, S], F32, name="ex_far%d" % t, align_bytes=64)
+            nc.vector.tensor_copy(ex_far[:], ex_win[t][:].indirect(n1_t[:]))
+            sum_ps.append(bank_b(t))
+            turn(sum_ps[t], every, ex_win[t], ex_far)
+            if t == 1:
+                logarithm(0)
+
+        w3_q = mx_tiles("w3")
+        w2_q = mx_tiles("w2")
+
+        def quantize_pair(operand, u, grouped):
+            quantize(operand, halves[u], grouped[:].rearrange("p t m j -> p (t m j)"))
+
+        w3_low = deal(w3_raw, 0, False, "ex_far1")
+        w2_low = deal(w2_raw, 0, False, "ex_far2")
+        quantize_pair(w3_q, 0, w3_low)
+        quantize_pair(w2_q, 0, w2_low)
+
+        last = PACK - 1
+        neg_z = sb.tile([P, PACK, S], F32, name="neg_z")
+        gy_win, glse = [], []
+
+        def subtract_far(t, cols):
+            lc = slice(cols.start // 16, cols.stop // 16)
+            nc.vector.tensor_tensor(neg_z[:, t, cols], gy_win[t][:].indirect(n2_t[:, lc]), glse[t][:, cols], ALU.subtract)
+
+        for t in range(PACK):
+            gy_win.append(sb.tile([P, WINDOW], F32, name="gy_win", tag="ex_win%d" % (t + 1) if t != last else "ex_far3", align_bytes=64))
             nc.scalar.activation(gy_win[t][:, :S], y_ps[t][:], ACT.Copy, scale=gain[:, t : t + 1])
             if t != last:
                 logarithm(t + 1)
@@ -170,10 +173,15 @@ def tile_picked_latecrossblse_none_p_kernel(tc, x_words, x_scales, w1, gn, w2, w
             nc.scalar.activation(glse[t][:], lse_ps[t][:], ACT.Copy, scale=gain[:, t : t + 1])
             if t != last:
                 subtract_far(t, every)
-        for t in range(PACK):
-            d_ps.append(bank_a(t))
+        d_ps = {}
+
+        def d_product(t):
+            d_ps.setdefault(t, bank_a(t) if t < 2 else bank_b(t - 2))
             product(d_ps[t], w3_q, t, x2, every)
-        w2_right = deal(w2_raw, 1, True, "lse_turned3")
+
+        d_product(0)
+        d_product(1)
+        w2_high = deal(w2_raw, 1, True, "lse_turned3")
 
         d_win = [sb.tile([P, WINDOW], F32, name="d_win%d" % t) for t in range(PACK)]
         h_win = [sb.tile([P, WINDOW], F32, name="h_win%d" % t) for t in range(PACK)]
@@ -186,36 +194,38 @@ def tile_picked_latecrossblse_none_p_kernel(tc, x_words, x_scales, w1, gn, w2, w
 
         z_q = mx_tiles("z")
 
-        def weave(cols):
-            woven = sb.tile([P, HALF, PACK], BF16, name="woven", align_bytes=64)
-            nc.vector.tensor_copy(
-                woven[:].rearrange("p (c i) t -> p c t i", i=4),
-                neg_z[:, :, cols].rearrange("p t (c i) -> p c t i", i=4),
-            )
+        def weave(cols, on_scalar):
+            woven = sb.tile([P, HALF, PACK], BF16, name="woven", tag="woven%d" % cols.start, align_bytes=64)
+            dst = woven[:].rearrange("p (c i) t -> p c t i", i=4)
+            src = neg_z[:, :, cols].rearrange("p t (c i) -> p c t i", i=4)
+            if on_scalar:
+                nc.scalar.activation(dst, src, ACT.Copy)
+            else:
+                nc.vector.tensor_copy(dst, src)
             return woven[:].rearrange("p c t -> p (c t)")
 
-        h_ps = {}
-
         def h_out(t, cols):
-            if t not in h_ps:
-                h_ps.setdefault(t, bank_b(t))
-            product(h_ps[t], w2_q, t, z_q, cols)
-            nc.scalar.activation(h_win[t][:, cols], h_ps[t][:, cols], ACT.Copy)
+            h_ps = bank_b(t) if cols.start == 0 else bank_a(t + 2)
+            product(h_ps, w2_q, t, z_q, cols)
+            nc.scalar.activation(h_win[t][:, cols], h_ps[:, cols], ACT.Copy)
 
+        for cols in halves:
+            subtract_far(last, cols)
+        quantize(z_q, left, weave(left, False))
+        quantize_pair(w2_q, 1, w2_high)
         d_out(0, False)
+        z_right = weave(right, True)
         d_out(0, True)
         d_out(1, False)
-        subtract_far(last, left)
-        z_left = weave(left)
-        subtract_far(last, right)
-        quantize(z_q, left, z_left)
+        w3_high = deal(w3_raw, 1, False, "woven0")
+        quantize(z_q, right, z_right)
+        quantize_pair(w3_q, 1, w3_high)
         h_out(0, left)
         h_out(1, left)
-        z_right = weave(right)
-        quantize(w2_q, right, w2_right[:].rearrange("p t m j -> p (t m j)"))
-        quantize(z_q, right, z_right)
         h_out(0, right)
         h_out(1, right)
+        d_product(2)
+        d_product(3)
         d_out(1, True)
 
         out_rows = out.rearrange("(p t) n -> t p n", t=PACK)
@@ -237,7 +247,7 @@ def tile_picked_latecrossblse_none_p_kernel(tc, x_words, x_scales, w1, gn, w2, w
 
         def add_terms(t, cols):
             if t not in turned_ps:
-                turned_ps.setdefault(t, bank_a(t))
+                turned_ps.setdefault(t, bank_a(t) if t < 2 else bank_b(0))
             turn(turned_ps[t], cols, first[t], second[t])
 
         def sum_out(t, cols):
@@ -245,7 +255,7 @@ def tile_picked_latecrossblse_none_p_kernel(tc, x_words, x_scales, w1, gn, w2, w
 
         def turn_back(t, cols):
             if t not in res_ps:
-                res_ps.setdefault(t, bank_b(t))
+                res_ps.setdefault(t, bank_a(t + 2) if t < 2 else bank_b(2))
             turn(res_ps[t], cols, turned[t])
 
         def store(t, cols):

from contextlib import ExitStack

import concourse.mybir as mybir
from concourse.masks import make_identity

K, T, S, H, N = 512, 2048, 512, 512, 512
FLOPS = 2 * S * (K * H + H * N + K * N)

F32 = mybir.dt.float32
BF16 = mybir.dt.bfloat16
I32 = mybir.dt.int32
U32 = mybir.dt.uint32
U16 = mybir.dt.uint16
U8 = mybir.dt.uint8
FP8X4 = mybir.dt.float8_e4m3fn_x4
ACT = mybir.ActivationFunctionType
ALU = mybir.AluOpType

P = 128
PACK = 4
HALF = S // 2
WINDOW = 2 * S


def tile_picked_latecrossblse_none_p_kernel(tc, x_words, x_scales, w1, gn, w2, w3, offs, n1, n2, two, n3, n4, out):
    nc = tc.nc
    with ExitStack() as ctx:
        sb = ctx.enter_context(tc.tile_pool(name="sb", bufs=1))
        psum = ctx.enter_context(tc.psum_pool(name="psum", bufs=1))

        def load_list(src, name):
            tile = sb.tile([P, S // 16], U16, name=name)
            nc.sync.dma_start(tile[:], src)
            return tile

        def load_weight(w, name):
            raw = sb.tile([P, PACK, S], F32, name=name)
            nc.sync.dma_start(raw[:], w.rearrange("(p j) c -> p j c", j=PACK))
            return raw

        scale_table = sb.tile([P, T], U8, name="scale_table")
        nc.gpsimd.memset(scale_table[:].bitcast(I32), 0)
        offs_t = load_list(offs, "offs_t")
        two_t = load_list(two, "two_t")
        for q in range(4):
            nc.sync.dma_start(scale_table[32 * q : 32 * q + 4, :].bitcast(I32), x_scales[0, 4 * q : 4 * q + 4, :].bitcast(I32))
        w1_raw = load_weight(w1, "w1_raw")
        word_table = sb.tile([P, T], I32, name="word_table")
        nc.sync.dma_start(word_table[:], x_words[0].rearrange("p n t -> p (n t)").bitcast(I32))
        n1_t = load_list(n1, "n1_t")
        gain = sb.tile([P, PACK], F32, name="gain")
        nc.sync.dma_start(gain[:], gn.rearrange("(p t) o -> p (t o)", t=PACK))
        w3_raw = load_weight(w3, "w3_raw")
        n2_t = load_list(n2, "n2_t")
        w2_raw = load_weight(w2, "w2_raw")
        n4_t = load_list(n4, "n4_t")
        n3_t = load_list(n3, "n3_t")
        identity = sb.tile([P, P], F32, name="identity")
        make_identity(nc, identity[:])

        def pick_scales(lst, name):
            picked = sb.tile([P, S], U8, name=name, align_bytes=64)
            nc.vector.tensor_copy(picked[:], scale_table[:].indirect(lst[:]))
            return picked

        def pick_words(lst, name, pieces):
            picked = sb.tile([P, S], U32, name=name, align_bytes=64)
            for cols in pieces:
                nc.vector.tensor_copy(picked[:, cols], word_table[:].bitcast(U32).indirect(lst[:, cols.start // 16 : cols.stop // 16]))
            return picked

        def deal(raw, u, on_scalar, tag):
            grouped = sb.tile([P, 2, P, PACK], BF16, name="grouped", tag=tag, align_bytes=64)
            dst = grouped[:].rearrange("p t m j -> p m j t")
            src = raw[:].rearrange("p j (m t) -> p m j t", t=PACK)[:, :, :, 2 * u : 2 * u + 2]
            if on_scalar:
                nc.scalar.activation(dst, src, ACT.Copy)
            else:
                nc.vector.tensor_copy(dst, src)
            return grouped

        def mx_tiles(name):
            codes = sb.tile([P, S], U32, name=name + "_codes", align_bytes=64)
            scales = sb.tile([P, S], U8, name=name + "_scales", align_bytes=64)
            return codes, scales

        def quantize(operand, cols, values):
            nc.vector.quantize_mx(out=operand[0][:, cols].bitcast(FP8X4), scales=operand[1][:, cols], in_=values)

        def product(acc, weights, t, moving, cols):
            rows = slice(t * P, (t + 1) * P)
            nc.tensor.matmul_mx(
                out=acc[:, cols],
                lhsT=weights[0][:, rows].bitcast(FP8X4), lhsT_scale=weights[1][:, rows],
                rhs=moving[0][:, cols].bitcast(FP8X4), rhs_scale=moving[1][:, cols],
                start=True, stop=True,
            )

        def turn(bank, span, *terms):
            for first_col in range(span.start, span.stop, P):
                cols = slice(first_col, first_col + P)
                for k, term in enumerate(terms):
                    nc.tensor.matmul(bank[:, cols], term[:, cols], identity[:], start=k == 0, stop=k == len(terms) - 1, is_transpose=True)

        def bank_a(t):
            return psum.tile([P, S], F32, name="bank_a%d" % t)

        def bank_b(t):
            return psum.tile([P, S], F32, name="bank_b%d" % t)

        every = slice(0, S)
        halves = [slice(0, HALF), slice(HALF, S)]

        x1_scales = pick_scales(offs_t, "x1_scales")
        x2_scales = pick_scales(two_t, "x2_scales")
        w1_g = [deal(w1_raw, 0, False, "w1_a"), deal(w1_raw, 1, True, "w1_b")]
        w1_q = mx_tiles("w1")
        for u in range(2):
            quantize(w1_q, halves[u], w1_g[u][:].rearrange("p t m j -> p (t m j)"))
        x1 = (pick_words(offs_t, "x1_words", halves), x1_scales)
        x2 = (pick_words(two_t, "x2_words", [every]), x2_scales)
        y_ps = [bank_a(t) for t in range(PACK)]
        ex_win, sum_ps = [], []
        left, right = halves
        for t in range(2):
            product(y_ps[t], w1_q, t, x1, left)
        for t in range(PACK):
            product(y_ps[t], w1_q, t, x1, right if t < 2 else every)
            ex_win.append(sb.tile([P, WINDOW], F32, name="ex_win%d" % t, align_bytes=64))
            nc.scalar.activation(ex_win[t][:, :S], y_ps[t][:], ACT.Exp)

        lse_ps = []

        def logarithm(t):
            lse_turned = sb.tile([P, S], F32, name="lse_turned%d" % t, align_bytes=64)
            nc.scalar.activation(lse_turned[:], sum_ps[t][:], ACT.Ln)
            lse_ps.append(bank_b(t))
            turn(lse_ps[t], every, lse_turned)

        for t in range(PACK):
            ex_far = sb.tile([P, S], F32, name="ex_far%d" % t, align_bytes=64)
            nc.vector.tensor_copy(ex_far[:], ex_win[t][:].indirect(n1_t[:]))
            sum_ps.append(bank_b(t))
            turn(sum_ps[t], every, ex_win[t], ex_far)
            if t == 1:
                logarithm(0)

        w3_q = mx_tiles("w3")
        w2_q = mx_tiles("w2")

        def quantize_pair(operand, u, grouped):
            quantize(operand, halves[u], grouped[:].rearrange("p t m j -> p (t m j)"))

        w3_low = deal(w3_raw, 0, False, "ex_far1")
        w2_low = deal(w2_raw, 0, False, "ex_far2")
        quantize_pair(w3_q, 0, w3_low)
        quantize_pair(w2_q, 0, w2_low)

        last = PACK - 1
        neg_z = sb.tile([P, PACK, S], F32, name="neg_z")
        gy_win, glse = [], []

        def subtract_far(t, cols):
            lc = slice(cols.start // 16, cols.stop // 16)
            nc.vector.tensor_tensor(neg_z[:, t, cols], gy_win[t][:].indirect(n2_t[:, lc]), glse[t][:, cols], ALU.subtract)

        for t in range(PACK):
            gy_win.append(sb.tile([P, WINDOW], F32, name="gy_win", tag="ex_win%d" % (t + 1) if t != last else "ex_far3", align_bytes=64))
            nc.scalar.activation(gy_win[t][:, :S], y_ps[t][:], ACT.Copy, scale=gain[:, t : t + 1])
            if t != last:
                logarithm(t + 1)
            glse.append(sb.tile([P, S], F32, name="glse%d" % t))
            nc.scalar.activation(glse[t][:], lse_ps[t][:], ACT.Copy, scale=gain[:, t : t + 1])
            if t != last:
                subtract_far(t, every)
        d_ps = {}

        def d_product(t):
            d_ps.setdefault(t, bank_a(t) if t < 2 else bank_b(t - 2))
            product(d_ps[t], w3_q, t, x2, every)

        d_product(0)
        d_product(1)
        w2_high = deal(w2_raw, 1, True, "lse_turned3")

        d_win = [sb.tile([P, WINDOW], F32, name="d_win%d" % t) for t in range(PACK)]
        h_win = [sb.tile([P, WINDOW], F32, name="h_win%d" % t) for t in range(PACK)]

        def d_out(t, negated):
            if negated:
                nc.scalar.activation(d_win[t][:, S:], d_ps[t][:], ACT.Copy, scale=0.75)
            else:
                nc.scalar.activation(d_win[t][:, :S], d_ps[t][:], ACT.Copy, scale=-0.75)

        z_q = mx_tiles("z")

        def weave(cols, on_scalar):
            woven = sb.tile([P, HALF, PACK], BF16, name="woven", tag="woven%d" % cols.start, align_bytes=64)
            dst = woven[:].rearrange("p (c i) t -> p c t i", i=4)
            src = neg_z[:, :, cols].rearrange("p t (c i) -> p c t i", i=4)
            if on_scalar:
                nc.scalar.activation(dst, src, ACT.Copy)
            else:
                nc.vector.tensor_copy(dst, src)
            return woven[:].rearrange("p c t -> p (c t)")

        def h_out(t, cols):
            h_ps = bank_b(t) if cols.start == 0 else bank_a(t + 2)
            product(h_ps, w2_q, t, z_q, cols)
            nc.scalar.activation(h_win[t][:, cols], h_ps[:, cols], ACT.Copy)

        for cols in halves:
            subtract_far(last, cols)
        quantize(z_q, left, weave(left, False))
        quantize_pair(w2_q, 1, w2_high)
        d_out(0, False)
        z_right = weave(right, True)
        d_out(0, True)
        d_out(1, False)
        w3_high = deal(w3_raw, 1, False, "woven0")
        quantize(z_q, right, z_right)
        quantize_pair(w3_q, 1, w3_high)
        h_out(0, left)
        h_out(1, left)
        h_out(0, right)
        h_out(1, right)
        d_product(2)
        d_product(3)
        d_out(1, True)

        out_rows = out.rearrange("(p t) n -> t p n", t=PACK)
        first = [sb.tile([P, S], F32, name="first%d" % t) for t in range(PACK)]
        second = [sb.tile([P, S], F32, name="second%d" % t) for t in range(PACK)]
        res = [sb.tile([P, S], F32, name="res%d" % t) for t in range(PACK)]

        def first_term(t, cols):
            lc = slice(cols.start // 16, cols.stop // 16)
            nc.vector.tensor_tensor(first[t][:, cols], d_win[t][:].indirect(n4_t[:, lc]), h_win[t][:, cols], ALU.mult)

        def second_term(t, cols):
            lc = slice(cols.start // 16, cols.stop // 16)
            shift = 0 if t == last else S
            nc.vector.tensor_tensor(second[t][:, cols], h_win[t][:].indirect(n3_t[:, lc]), d_win[t][:, shift + cols.start : shift + cols.stop], ALU.mult)

        turned = [sb.tile([P, S], F32, name="turned%d" % t) for t in range(last)]
        turned_ps, res_ps = {}, {}

        def add_terms(t, cols):
            if t not in turned_ps:
                turned_ps.setdefault(t, bank_a(t) if t < 2 else bank_b(0))
            turn(turned_ps[t], cols, first[t], second[t])

        def sum_out(t, cols):
            nc.scalar.activation(turned[t][:, cols], turned_ps[t][:, cols], ACT.Copy)

        def turn_back(t, cols):
            if t not in res_ps:
                res_ps.setdefault(t, bank_a(t + 2) if t < 2 else bank_b(2))
            turn(res_ps[t], cols, turned[t])

        def store(t, cols):
            nc.scalar.activation(res[t][:, cols], res_ps[t][:, cols], ACT.Copy)
            nc.scalar.dma_start(out_rows[t][:, cols], res[t][:, cols])

        d_out(2, False)
        d_out(2, True)
        h_out(2, every)
        d_out(3, False)
        h_out(3, every)
        first_term(0, left)
        first_term(1, left)
        first_term(0, right)
        second_term(0, every)
        first_term(1, right)
        second_term(1, every)
        for cols in halves:
            first_term(2, cols)
            second_term(2, cols)
        first_term(3, every)
        for cols in halves:
            second_term(3, cols)
        for cols in halves:
            nc.vector.tensor_tensor(res[3][:, cols], first[3][:, cols], second[3][:, cols], ALU.subtract)
        add_terms(0, every)
        sum_out(0, every)
        add_terms(1, every)
        turn_back(0, every)
        sum_out(1, every)
        store(0, every)
        add_terms(2, left)
        turn_back(1, every)
        sum_out(2, left)
        store(1, every)
        add_terms(2, right)
        turn_back(2, left)
        sum_out(2, right)
        store(2, left)
        turn_back(2, right)
        store(2, right)
        for cols in halves:
            nc.sync.dma_start(out_rows[3][:, cols], res[3][:, cols])
